import numpy as np
import ml_dtypes


def mxq(x, axis, fmt="e4m3"):
    dtype, down = {"e4m3": (ml_dtypes.float8_e4m3fn, 7), "e5m2": (ml_dtypes.float8_e5m2, 14)}[fmt]
    v = np.moveaxis(np.asarray(x, np.float32).astype(ml_dtypes.bfloat16).astype(np.float64), axis, -1)
    blocks = v.reshape(v.shape[:-1] + (-1, 32))
    amax = np.abs(blocks).max(-1, keepdims=True)
    byte = np.maximum(np.where(amax > 0, np.frexp(amax)[1] - 1 + 127, 0) - down, 1)
    scale = np.exp2(byte - 127.0)
    codes = (blocks / scale).astype(np.float32).astype(dtype).astype(np.float64)
    return np.moveaxis((codes * scale).reshape(v.shape), -1, axis)


WIDE = False


def mx_kscale(k):
    if not WIDE:
        return np.ones(k)
    levels = np.array([10, -10, 5, -5, 0])
    if k % 512:
        return np.exp2(np.random.permutation(np.resize(levels, k // 32))).repeat(32)
    a = np.empty((k // 512, 16))
    for p in range(k // 512):
        a[p, :8] = np.random.permutation(np.resize(levels, 8))
        for g in range(8):
            far = levels[np.abs(levels - a[p, g]) >= 10]
            a[p, g + 8] = far[np.random.randint(len(far))]
    return np.exp2(a.ravel()).repeat(32)


def f64(x):
    return np.asarray(x).astype(np.float64)


def striped(idx):
    return np.tile(np.asarray(idx).reshape(-1, 16).T, (8, 1)).astype(np.uint16)


def unstriped(offs):
    return offs[:16].T.reshape(-1).astype(np.int64)


E2M1 = np.array([0.0, 0.5, 1.0, 1.5, 2.0, 3.0, 4.0, 6.0, -0.0, -0.5, -1.0, -1.5, -2.0, -3.0, -4.0, -6.0])


def pack_weight(w, fmt):
    k, n = w.shape
    w = f64(np.asarray(w, np.float32).astype(ml_dtypes.bfloat16)).reshape(k // 32, 32, n)
    amax = np.abs(w).max(1)
    if fmt == "e4m3":
        byte = np.frexp(amax)[1] - 1 + 127 - 7
    else:
        mant, ex = np.frexp(amax / 6.0)
        byte = np.where(mant > 0.5, ex, ex - 1) + 127
    byte = np.clip(np.where(amax > 0, byte, 1), 1, 254)
    scaled = (w * np.exp2(127.0 - byte)[:, None, :]).reshape(k, n).astype(np.float32)
    by_word = np.ascontiguousarray(scaled.reshape(k // 512, 128, 4, n).transpose(0, 1, 3, 2))
    if fmt == "e4m3":
        words = by_word.astype(ml_dtypes.float8_e4m3fn).view(np.uint8)
    else:
        c = by_word.astype(ml_dtypes.float4_e2m1fn).view(np.uint8) & 0xF
        words = (c[..., 0::2] | (c[..., 1::2] << 4)).reshape(k // 512, 128, 2 * n)
    return np.ascontiguousarray(words), np.ascontiguousarray(byte.astype(np.uint8).reshape(k // 512, 16, n))


def unpack_weight(words, scales, fmt):
    g, _, n = scales.shape
    words = np.ascontiguousarray(words).reshape(g, 128, n, -1)
    if fmt == "e4m3":
        vals = words.view(ml_dtypes.float8_e4m3fn).astype(np.float64)
    else:
        nib = np.empty((g, 128, n, 4), np.uint8)
        nib[..., 0::2] = words & 0xF
        nib[..., 1::2] = words >> 4
        vals = E2M1[nib]
    vals = vals * np.repeat(np.exp2(scales.astype(np.float64) - 127.0), 8, axis=1)[..., None]
    return vals.transpose(0, 1, 3, 2).reshape(g * 512, n)


K, I, L, S, T, N = 1024, 512, 512, 512, 512, 512


def setup_inputs():
    n = np.random.standard_normal
    idx = np.random.randint(0, I, T)
    idx2 = np.random.randint(0, S, T)
    fk = mx_kscale(K)
    fl = mx_kscale(L)
    xap = pack_weight(n((K, I)) / fk[:, None], "e4m3")
    xbp = pack_weight(n((L, S)) / fl[:, None], "e2m1")
    wbp = pack_weight(n((L, N)) * 1 / np.sqrt(L) * fl[:, None], "e4m3")
    return {
        "xa_words": xap[0],
        "xa_scales": xap[1],
        "wa": (n((K, N)) * 1 / np.sqrt(K) * fk[:, None]).astype(np.float32),
        "xb_words": xbp[0],
        "xb_scales": xbp[1],
        "wb_words": wbp[0],
        "wb_scales": wbp[1],
        "res": (1.0 * n((N, T))).astype(np.float32),
        "offs": striped(idx),
        "offs2": striped(idx2),
    }


def reference(xa_words, xa_scales, wa, xb_words, xb_scales, wb_words, wb_scales, res, offs, offs2):
    idx = unstriped(offs)
    idx2 = unstriped(offs2)
    xau = unpack_weight(xa_words, xa_scales, "e4m3")
    xbu = unpack_weight(xb_words, xb_scales, "e2m1")
    wbu = unpack_weight(wb_words, wb_scales, "e4m3")
    waq = mxq(f64(wa), 0, "e4m3")
    za = waq.T @ xau
    zb = wbu.T @ xbu
    y = np.maximum(za[:, idx], zb[:, idx2]) - 0.25 * np.square(za[:, idx] - zb[:, idx2]) + 0.3 * f64(res)
    return y

@@ -1,0 +1,171 @@
+from contextlib import ExitStack
+
+import concourse.mybir as mybir
+
+K, I, L, S, T, N = 1024, 512, 512, 512, 512, 512
+FLOPS = 2 * K * N * I + 2 * L * N * S
+
+F32 = mybir.dt.float32
+BF16 = mybir.dt.bfloat16
+I32 = mybir.dt.int32
+U32 = mybir.dt.uint32
+U16 = mybir.dt.uint16
+U8 = mybir.dt.uint8
+FP8X4 = mybir.dt.float8_e4m3fn_x4
+FP4X4 = mybir.dt.float4_e2m1fn_x4
+ALU = mybir.AluOpType
+ACT = mybir.ActivationFunctionType
+
+P = 128
+PACK = 4
+K_PASS = P * PACK
+PASSES = K // K_PASS
+BLOCKS = N // P
+HALF = N // 2
+
+
+def tile_moe_combine_by_larger_kernel(
+    tc, xa_words, xa_scales, wa, xb_words, xb_scales, wb_words, wb_scales, res, offs, offs2, out
+):
+    nc = tc.nc
+    with ExitStack() as ctx:
+        held = ctx.enter_context(tc.tile_pool(name="held", bufs=1))
+        psum = ctx.enter_context(tc.psum_pool(name="psum", bufs=1))
+
+        list_a = held.tile([P, T // 16], U16, name="list_a")
+        list_b = held.tile([P, T // 16], U16, name="list_b")
+        wb_w = held.tile([P, PACK * N], U8, name="wb_w", align_bytes=64)
+        xb_w = held.tile([P, 2 * S], U8, name="xb_w", align_bytes=64)
+        xa_w = held.tile([P, PASSES, PACK * I], U8, name="xa_w", align_bytes=64)
+        wb_s = held.tile([P, N], U8, name="wb_s", align_bytes=64)
+        xb_s = held.tile([P, S], U8, name="xb_s", align_bytes=64)
+        xa_s = held.tile([P, PASSES, I], U8, name="xa_s", align_bytes=64)
+        wa_raw = [held.tile([P, PASSES, PACK, HALF], F32, name="wa_raw%d" % h) for h in range(2)]
+        res_sb = [held.tile([P, 2, T], F32, name="res%d" % h) for h in range(2)]
+
+        nc.vector.memset(wb_s[:].bitcast(I32), 0)
+        nc.vector.memset(xb_s[:].bitcast(I32), 0)
+        nc.vector.memset(xa_s[:].rearrange("p z c -> p (z c)").bitcast(I32), 0)
+
+        def load_wa(h):
+            for z in range(PASSES):
+                rows = wa[z * K_PASS : (z + 1) * K_PASS, h * HALF : (h + 1) * HALF]
+                nc.sync.dma_start(out=wa_raw[h][:, z, :, :], in_=rows.rearrange("(p j) n -> p j n", j=PACK))
+
+        def load_res(h):
+            rows = res[h * HALF : (h + 1) * HALF, :]
+            nc.sync.dma_start(out=res_sb[h][:], in_=rows.rearrange("(j p) t -> p j t", p=P))
+
+        nc.sync.dma_start(out=wb_w[:].bitcast(I32), in_=wb_words[0].rearrange("p n r -> p (n r)").bitcast(I32))
+        nc.sync.dma_start(out=xb_w[:].bitcast(I32), in_=xb_words[0].bitcast(I32))
+        for r in range(4):
+            nc.sync.dma_start(out=wb_s[r:P:32, :].bitcast(I32), in_=wb_scales[0, r:16:4, :].bitcast(I32))
+        for r in range(4):
+            nc.sync.dma_start(out=xb_s[r:P:32, :].bitcast(I32), in_=xb_scales[0, r:16:4, :].bitcast(I32))
+        nc.sync.dma_start(list_b[:], offs2)
+        load_wa(0)
+        nc.sync.dma_start(
+            out=xa_w[:].bitcast(I32), in_=xa_words.rearrange("z p c r -> p z (c r)").bitcast(I32)
+        )
+        for r in range(4):
+            nc.sync.dma_start(
+                out=xa_s[r:P:32, :, :].bitcast(I32),
+                in_=xa_scales[:, r:16:4, :].rearrange("z q c -> q z c").bitcast(I32),
+            )
+        nc.sync.dma_start(list_a[:], offs)
+        load_res(0)
+        load_wa(1)
+        load_res(1)
+
+        z_sb = [held.tile([P, I + S], F32, name="z%d" % j) for j in range(BLOCKS)]
+        b_sb = [held.tile([P, T], F32, name="b%d" % j) for j in range(BLOCKS)]
+        d_sb = [held.tile([P, T], F32, name="d%d" % j) for j in range(BLOCKS)]
+        u_sb = [held.tile([P, T], F32, name="u%d" % j) for j in range(BLOCKS)]
+        w_sb = [held.tile([P, T], F32, name="w%d" % j) for j in range(BLOCKS)]
+        q_sb = [held.tile([P, T], F32, name="q%d" % j) for j in range(BLOCKS)]
+        y_sb = [held.tile([P, T], F32, name="y%d" % j) for j in range(BLOCKS)]
+
+        def product_b(j):
+            acc = psum.tile([P, S], F32, name="acc_b%d" % j)
+            nc.tensor.matmul_mx(
+                out=acc[:],
+                lhsT=wb_w[:, j * PACK * P : (j + 1) * PACK * P].bitcast(FP8X4),
+                lhsT_scale=wb_s[:, j * P : (j + 1) * P],
+                rhs=xb_w[:].bitcast(FP4X4),
+                rhs_scale=xb_s[:],
+                start=True,
+                stop=True,
+            )
+            nc.scalar.activation(z_sb[j][:, I : I + S], acc[:], ACT.Copy)
+
+        def gather_b(j):
+            for h in range(2):
+                nc.vector.tensor_copy(
+                    b_sb[j][:, h * T // 2 : (h + 1) * T // 2],
+                    z_sb[j][:, I : I + S].indirect(list_b[:, h * T // 32 : (h + 1) * T // 32]),
+                )
+
+        grouped = [held.tile([P, PASSES, P, PACK], BF16, name="grouped%d" % j, align_bytes=64) for j in range(BLOCKS)]
+        codes = [held.tile([P, PASSES * P], U32, name="codes%d" % j, align_bytes=64) for j in range(BLOCKS)]
+        scales = [held.tile([P, PASSES * P], U8, name="scales%d" % j, align_bytes=64) for j in range(BLOCKS)]
+
+        def round_wa(j):
+            src = wa_raw[j // 2][:, :, :, (j % 2) * P : (j % 2 + 1) * P]
+            nc.scalar.copy(
+                grouped[j][:].rearrange("p z (c i) t -> p z c t i", i=4),
+                src.rearrange("p z t (c i) -> p z c t i", i=4),
+            )
+
+        def quantize_wa(j):
+            nc.vector.quantize_mx(
+                out=codes[j][:].bitcast(FP8X4),
+                scales=scales[j][:],
+                in_=grouped[j][:].rearrange("p z n t -> p (z n t)"),
+            )
+
+        def product_a(j):
+            acc = psum.tile([P, I], F32, name="acc_a%d" % j)
+            for z in range(PASSES):
+                nc.tensor.matmul_mx(
+                    out=acc[:],
+                    lhsT=codes[j][:, z * P : (z + 1) * P].bitcast(FP8X4),
+                    lhsT_scale=scales[j][:, z * P : (z + 1) * P],
+                    rhs=xa_w[:, z, :].bitcast(FP8X4),
+                    rhs_scale=xa_s[:, z, :],
+                    start=(z == 0),
+                    stop=(z == PASSES - 1),
+                )
+            nc.scalar.activation(z_sb[j][:, 0:I], acc[:], ACT.Copy)
+
+        def base(j):
+            nc.vector.scalar_tensor_tensor(
+                u_sb[j][:], res_sb[j // 2][:, j % 2, :], 0.3, b_sb[j][:], ALU.mult, ALU.add
+            )
+
+        def gap(j):
+            nc.vector.tensor_tensor(d_sb[j][:], z_sb[j][:].indirect(list_a[:]), b_sb[j][:], ALU.subtract)
+            nc.scalar.activation(q_sb[j][:], d_sb[j][:], ACT.Square, scale=0.5)
+
+        def larger(j):
+            nc.vector.scalar_tensor_tensor(w_sb[j][:], d_sb[j][:], 0.0, u_sb[j][:], ALU.max, ALU.add)
+
+        def finish(j):
+            nc.vector.tensor_tensor(y_sb[j][:], w_sb[j][:], q_sb[j][:], ALU.subtract)
+            nc.sync.dma_start(out=out[j * P : (j + 1) * P, :], in_=y_sb[j][:])
+
+        for j in range(BLOCKS):
+            product_b(j)
+            gather_b(j)
+        for j in range(BLOCKS):
+            round_wa(j)
+            quantize_wa(j)
+            if j > 0:
+                product_a(j - 1)
+        product_a(BLOCKS - 1)
+        for j in range(BLOCKS):
+            gap(j)
+            if j > 0:
+                finish(j - 1)
+            base(j)
+            larger(j)
+        finish(BLOCKS - 1)

@@ -1,6 +1,7 @@
 from contextlib import ExitStack
 
 import concourse.mybir as mybir
+from concourse.masks import make_identity
 
 K, I, L, S, T, N = 1024, 512, 512, 512, 512, 512
 FLOPS = 2 * K * N * I + 2 * L * N * S
@@ -22,6 +23,7 @@ K_PASS = P * PACK
 PASSES = K // K_PASS
 BLOCKS = N // P
 HALF = N // 2
+RES_GAIN = 0.3
 
 
 def tile_moe_combine_by_larger_kernel(
@@ -37,14 +39,14 @@ def tile_moe_combine_by_larger_kernel(
         wb_w = held.tile([P, PACK * N], U8, name="wb_w", align_bytes=64)
         xb_w = held.tile([P, 2 * S], U8, name="xb_w", align_bytes=64)
         xa_w = held.tile([P, PASSES, PACK * I], U8, name="xa_w", align_bytes=64)
-        wb_s = held.tile([P, N], U8, name="wb_s", align_bytes=64)
-        xb_s = held.tile([P, S], U8, name="xb_s", align_bytes=64)
+        b_planes = held.tile([P, N + S], U8, name="b_planes", align_bytes=64)
         xa_s = held.tile([P, PASSES, I], U8, name="xa_s", align_bytes=64)
-        wa_raw = [held.tile([P, PASSES, PACK, HALF], F32, name="wa_raw%d" % h) for h in range(2)]
+        wa_raw = [held.tile([P, PASSES, PACK, HALF], F32, name="wa_raw%d" % h, tag="raw%d" % h) for h in range(2)]
         res_sb = [held.tile([P, 2, T], F32, name="res%d" % h) for h in range(2)]
 
-        nc.vector.memset(wb_s[:].bitcast(I32), 0)
-        nc.vector.memset(xb_s[:].bitcast(I32), 0)
+        ident = held.tile([P, P], F32, name="ident")
+        make_identity(nc, ident[:])
+        nc.vector.memset(b_planes[:].bitcast(I32), 0)
         nc.vector.memset(xa_s[:].rearrange("p z c -> p (z c)").bitcast(I32), 0)
 
         def load_wa(h):
@@ -59,9 +61,9 @@ def tile_moe_combine_by_larger_kernel(
         nc.sync.dma_start(out=wb_w[:].bitcast(I32), in_=wb_words[0].rearrange("p n r -> p (n r)").bitcast(I32))
         nc.sync.dma_start(out=xb_w[:].bitcast(I32), in_=xb_words[0].bitcast(I32))
         for r in range(4):
-            nc.sync.dma_start(out=wb_s[r:P:32, :].bitcast(I32), in_=wb_scales[0, r:16:4, :].bitcast(I32))
+            nc.sync.dma_start(out=b_planes[r:P:32, 0:N].bitcast(I32), in_=wb_scales[0, r:16:4, :].bitcast(I32))
         for r in range(4):
-            nc.sync.dma_start(out=xb_s[r:P:32, :].bitcast(I32), in_=xb_scales[0, r:16:4, :].bitcast(I32))
+            nc.sync.dma_start(out=b_planes[r:P:32, N : N + S].bitcast(I32), in_=xb_scales[0, r:16:4, :].bitcast(I32))
         nc.sync.dma_start(list_b[:], offs2)
         load_wa(0)
         nc.sync.dma_start(
@@ -72,40 +74,41 @@ def tile_moe_combine_by_larger_kernel(
                 out=xa_s[r:P:32, :, :].bitcast(I32),
                 in_=xa_scales[:, r:16:4, :].rearrange("z q c -> q z c").bitcast(I32),
             )
+        load_wa(1)
         nc.sync.dma_start(list_a[:], offs)
         load_res(0)
-        load_wa(1)
         load_res(1)
 
-        z_sb = [held.tile([P, I + S], F32, name="z%d" % j) for j in range(BLOCKS)]
-        b_sb = [held.tile([P, T], F32, name="b%d" % j) for j in range(BLOCKS)]
-        d_sb = [held.tile([P, T], F32, name="d%d" % j) for j in range(BLOCKS)]
-        u_sb = [held.tile([P, T], F32, name="u%d" % j) for j in range(BLOCKS)]
+        zb_sb = [held.tile([P, S], F32, name="zb%d" % j) for j in range(BLOCKS)]
+        za_sb = {}
+        b_sb = {}
+        u_sb = [held.tile([P, T], F32, name="u%d" % j, tag="u%d" % j, align_bytes=64) for j in range(BLOCKS)]
         w_sb = [held.tile([P, T], F32, name="w%d" % j) for j in range(BLOCKS)]
-        q_sb = [held.tile([P, T], F32, name="q%d" % j) for j in range(BLOCKS)]
         y_sb = [held.tile([P, T], F32, name="y%d" % j) for j in range(BLOCKS)]
 
         def product_b(j):
-            acc = psum.tile([P, S], F32, name="acc_b%d" % j)
+            acc = psum.tile([P, S], F32, name="acc_b%d" % j, tag="bank%d" % j)
             nc.tensor.matmul_mx(
                 out=acc[:],
                 lhsT=wb_w[:, j * PACK * P : (j + 1) * PACK * P].bitcast(FP8X4),
-                lhsT_scale=wb_s[:, j * P : (j + 1) * P],
+                lhsT_scale=b_planes[:, j * P : (j + 1) * P],
                 rhs=xb_w[:].bitcast(FP4X4),
-                rhs_scale=xb_s[:],
+                rhs_scale=b_planes[:, N : N + S],
                 start=True,
                 stop=True,
             )
-            nc.scalar.activation(z_sb[j][:, I : I + S], acc[:], ACT.Copy)
+            nc.scalar.activation(zb_sb[j][:], acc[:], ACT.Copy, scale=1.0 / RES_GAIN)
 
         def gather_b(j):
+            tag = "slot0" if j == BLOCKS - 1 else "b%d" % j
+            b_sb[j] = held.tile([P, T], F32, name="b%d" % j, tag=tag, align_bytes=64)
             for h in range(2):
                 nc.vector.tensor_copy(
                     b_sb[j][:, h * T // 2 : (h + 1) * T // 2],
-                    z_sb[j][:, I : I + S].indirect(list_b[:, h * T // 32 : (h + 1) * T // 32]),
+                    zb_sb[j][:].indirect(list_b[:, h * T // 32 : (h + 1) * T // 32]),
                 )
 
-        grouped = [held.tile([P, PASSES, P, PACK], BF16, name="grouped%d" % j, align_bytes=64) for j in range(BLOCKS)]
+        grouped = [held.tile([P, PASSES, P, PACK], BF16, name="grouped%d" % j, tag="slot%d" % j, align_bytes=64) for j in range(BLOCKS)]
         codes = [held.tile([P, PASSES * P], U32, name="codes%d" % j, align_bytes=64) for j in range(BLOCKS)]
         scales = [held.tile([P, PASSES * P], U8, name="scales%d" % j, align_bytes=64) for j in range(BLOCKS)]
 
@@ -123,8 +126,10 @@ def tile_moe_combine_by_larger_kernel(
                 in_=grouped[j][:].rearrange("p z n t -> p (z n t)"),
             )
 
+        acc_a = {}
+
         def product_a(j):
-            acc = psum.tile([P, I], F32, name="acc_a%d" % j)
+            acc = psum.tile([P, I], F32, name="acc_a%d" % j, tag="bank%d" % (4 + j % 2))
             for z in range(PASSES):
                 nc.tensor.matmul_mx(
                     out=acc[:],
@@ -135,37 +140,87 @@ def tile_moe_combine_by_larger_kernel(
                     start=(z == 0),
                     stop=(z == PASSES - 1),
                 )
-            nc.scalar.activation(z_sb[j][:, 0:I], acc[:], ACT.Copy)
+            acc_a[j] = acc
+
+        def evacuate_a(j):
+            za_sb[j] = held.tile([P, I], F32, name="za%d" % j, tag="raw1" if j == 1 else "za%d" % j)
+            nc.scalar.activation(za_sb[j][:], acc_a[j][:], ACT.Copy, scale=1.0 / RES_GAIN)
+
+        u_ps = {}
 
         def base(j):
-            nc.vector.scalar_tensor_tensor(
-                u_sb[j][:], res_sb[j // 2][:, j % 2, :], 0.3, b_sb[j][:], ALU.mult, ALU.add
-            )
+            if j < 2:
+                nc.vector.tensor_tensor(u_sb[j][:], res_sb[j // 2][:, j % 2, :], b_sb[j][:], ALU.add)
+                u_ps[j] = u_sb[j]
+                return
+            turned = psum.tile([P, T], F32, name="turned%d" % j, tag="bank%d" % (6 + j % 2))
+            for c in range(T // P):
+                cols = slice(c * P, (c + 1) * P)
+                nc.tensor.matmul(
+                    turned[:, cols], res_sb[j // 2][:, j % 2, cols], ident[:], start=True, stop=False, is_transpose=True
+                )
+                nc.tensor.matmul(turned[:, cols], b_sb[j][:, cols], ident[:], start=False, stop=True, is_transpose=True)
+            nc.scalar.copy(u_sb[j][:], turned[:])
+            u_ps[j] = psum.tile([P, T], F32, name="u_ps%d" % j, tag="bank%d" % j)
+            for c in range(T // P):
+                cols = slice(c * P, (c + 1) * P)
+                nc.tensor.transpose(u_ps[j][:, cols], u_sb[j][:, cols], ident[:])
+
+        d_sb = {}
+        q_sb = {}
+        q_tags = ("slot3", "q1", "u2", "u3")
 
         def gap(j):
-            nc.vector.tensor_tensor(d_sb[j][:], z_sb[j][:].indirect(list_a[:]), b_sb[j][:], ALU.subtract)
-            nc.scalar.activation(q_sb[j][:], d_sb[j][:], ACT.Square, scale=0.5)
+            d_sb[j] = held.tile([P, T], F32, name="d%d" % j, tag="slot1" if j == 0 else "d%d" % j, align_bytes=64)
+            for h in range(2):
+                cols = slice(h * T // 2, (h + 1) * T // 2)
+                nc.vector.tensor_tensor(
+                    d_sb[j][:, cols],
+                    za_sb[j][:].indirect(list_a[:, h * T // 32 : (h + 1) * T // 32]),
+                    b_sb[j][:, cols],
+                    ALU.subtract,
+                )
+            q_sb[j] = held.tile([P, T], F32, name="q%d" % j, tag=q_tags[j], align_bytes=64)
+            nc.scalar.activation(q_sb[j][:], d_sb[j][:], ACT.Square, scale=0.5 * RES_GAIN)
 
-        def larger(j):
-            nc.vector.scalar_tensor_tensor(w_sb[j][:], d_sb[j][:], 0.0, u_sb[j][:], ALU.max, ALU.add)
+        def larger(j, cols=slice(0, T)):
+            nc.vector.scalar_tensor_tensor(w_sb[j][:, cols], d_sb[j][:, cols], 0.0, u_ps[j][:, cols], ALU.max, ALU.add)
 
-        def finish(j):
-            nc.vector.tensor_tensor(y_sb[j][:], w_sb[j][:], q_sb[j][:], ALU.subtract)
-            nc.sync.dma_start(out=out[j * P : (j + 1) * P, :], in_=y_sb[j][:])
+        def finish(j, cols=slice(0, T)):
+            nc.vector.scalar_tensor_tensor(
+                y_sb[j][:, cols], w_sb[j][:, cols], RES_GAIN, q_sb[j][:, cols], ALU.mult, ALU.subtract
+            )
+            nc.sync.dma_start(out=out[j * P : (j + 1) * P, cols], in_=y_sb[j][:, cols])
 
-        for j in range(BLOCKS):
+        for j in range(BLOCKS - 1):
             product_b(j)
             gather_b(j)
-        for j in range(BLOCKS):
+        round_wa(0)
+        quantize_wa(0)
+        product_b(BLOCKS - 1)
+        gather_b(BLOCKS - 1)
+        for j in range(1, BLOCKS):
             round_wa(j)
             quantize_wa(j)
-            if j > 0:
-                product_a(j - 1)
+            product_a(j - 1)
+            if j == 1:
+                evacuate_a(0)
         product_a(BLOCKS - 1)
         for j in range(BLOCKS):
+            if j + 1 < BLOCKS:
+                evacuate_a(j + 1)
+            if j == 0:
+                base(2)
+                base(3)
             gap(j)
             if j > 0:
                 finish(j - 1)
-            base(j)
-            larger(j)
-        finish(BLOCKS - 1)
+            if j < 2:
+                base(j)
+            if j < BLOCKS - 1:
+                larger(j)
+        halves = (slice(0, T // 2), slice(T // 2, T))
+        for cols in halves:
+            larger(BLOCKS - 1, cols)
+        for cols in halves:
+            finish(BLOCKS - 1, cols)

@@ -24,6 +24,7 @@ PASSES = K // K_PASS
 BLOCKS = N // P
 HALF = N // 2
 RES_GAIN = 0.3
+SPARE = 192
 
 
 def tile_moe_combine_by_larger_kernel(
@@ -41,50 +42,55 @@ def tile_moe_combine_by_larger_kernel(
         xa_w = held.tile([P, PASSES, PACK * I], U8, name="xa_w", align_bytes=64)
         b_planes = held.tile([P, N + S], U8, name="b_planes", align_bytes=64)
         xa_s = held.tile([P, PASSES, I], U8, name="xa_s", align_bytes=64)
-        wa_raw = [held.tile([P, PASSES, PACK, HALF], F32, name="wa_raw%d" % h, tag="raw%d" % h) for h in range(2)]
+        wa_raw = [held.tile([P, PASSES, PACK, HALF], F32, name="wa_raw%d" % h, tag="raw%d" % h, align_bytes=64) for h in range(2)]
         res_sb = [held.tile([P, 2, T], F32, name="res%d" % h) for h in range(2)]
 
         ident = held.tile([P, P], F32, name="ident")
-        make_identity(nc, ident[:])
         nc.vector.memset(b_planes[:].bitcast(I32), 0)
         nc.vector.memset(xa_s[:].rearrange("p z c -> p (z c)").bitcast(I32), 0)
+        make_identity(nc, ident[:])
 
-        def load_wa(h):
-            for z in range(PASSES):
-                rows = wa[z * K_PASS : (z + 1) * K_PASS, h * HALF : (h + 1) * HALF]
-                nc.sync.dma_start(out=wa_raw[h][:, z, :, :], in_=rows.rearrange("(p j) n -> p j n", j=PACK))
+        def load_words_b():
+            nc.sync.dma_start(out=wb_w[:].bitcast(I32), in_=wb_words[0].rearrange("p n r -> p (n r)").bitcast(I32))
+            nc.sync.dma_start(out=xb_w[:].bitcast(I32), in_=xb_words[0].bitcast(I32))
+
+        def load_scale_rows(plane, rows, queues=(nc.sync,) * 4):
+            for r in range(4):
+                queues[r].dma_start(out=plane[r:P:32].bitcast(I32), in_=rows[r:16:4].bitcast(I32))
+
+        def load_wa(h, z):
+            rows = wa[z * K_PASS : (z + 1) * K_PASS, h * HALF : (h + 1) * HALF]
+            nc.sync.dma_start(out=wa_raw[h][:, z, :, :], in_=rows.rearrange("(p j) n -> p j n", j=PACK))
 
         def load_res(h):
             rows = res[h * HALF : (h + 1) * HALF, :]
             nc.sync.dma_start(out=res_sb[h][:], in_=rows.rearrange("(j p) t -> p j t", p=P))
 
-        nc.sync.dma_start(out=wb_w[:].bitcast(I32), in_=wb_words[0].rearrange("p n r -> p (n r)").bitcast(I32))
-        nc.sync.dma_start(out=xb_w[:].bitcast(I32), in_=xb_words[0].bitcast(I32))
-        for r in range(4):
-            nc.sync.dma_start(out=b_planes[r:P:32, 0:N].bitcast(I32), in_=wb_scales[0, r:16:4, :].bitcast(I32))
-        for r in range(4):
-            nc.sync.dma_start(out=b_planes[r:P:32, N : N + S].bitcast(I32), in_=xb_scales[0, r:16:4, :].bitcast(I32))
+        load_words_b()
+        load_scale_rows(b_planes[:, 0:N], wb_scales[0])
+        load_wa(0, 0)
+        load_wa(0, 1)
+        load_scale_rows(b_planes[:, N : N + S], xb_scales[0])
         nc.sync.dma_start(list_b[:], offs2)
-        load_wa(0)
-        nc.sync.dma_start(
-            out=xa_w[:].bitcast(I32), in_=xa_words.rearrange("z p c r -> p z (c r)").bitcast(I32)
-        )
-        for r in range(4):
-            nc.sync.dma_start(
-                out=xa_s[r:P:32, :, :].bitcast(I32),
-                in_=xa_scales[:, r:16:4, :].rearrange("z q c -> q z c").bitcast(I32),
-            )
-        load_wa(1)
-        nc.sync.dma_start(list_a[:], offs)
+        load_wa(1, 0)
         load_res(0)
+        load_wa(1, 1)
+        nc.sync.dma_start(out=xa_w[:].bitcast(I32), in_=xa_words.rearrange("z p c r -> p z (c r)").bitcast(I32))
+        load_scale_rows(xa_s[:], xa_scales.rearrange("z q c -> q z c"))
+        nc.sync.dma_start(list_a[:], offs)
         load_res(1)
 
-        zb_sb = [held.tile([P, S], F32, name="zb%d" % j) for j in range(BLOCKS)]
-        za_sb = {}
-        b_sb = {}
-        u_sb = [held.tile([P, T], F32, name="u%d" % j, tag="u%d" % j, align_bytes=64) for j in range(BLOCKS)]
-        w_sb = [held.tile([P, T], F32, name="w%d" % j) for j in range(BLOCKS)]
-        y_sb = [held.tile([P, T], F32, name="y%d" % j) for j in range(BLOCKS)]
+        tags = {"u0":"codes1","u1":"codes3","q0":"codes3","q1":"u2","q2":"u3","q3":"d2"}
+        tiles = {}
+
+        def sb(name, j, width=T):
+            key = "%s%d" % (name, j)
+            if key not in tiles:
+                tiles[key] = held.tile([P, width], F32, name=key, tag=tags.get(key, key), align_bytes=64)
+            return tiles[key]
+
+        for j in range(BLOCKS):
+            nc.gpsimd.memset(sb("z", j, I + S + SPARE)[:, I + S :], 0.0)
 
         def product_b(j):
             acc = psum.tile([P, S], F32, name="acc_b%d" % j, tag="bank%d" % j)
@@ -97,27 +103,29 @@ def tile_moe_combine_by_larger_kernel(
                 start=True,
                 stop=True,
             )
-            nc.scalar.activation(zb_sb[j][:], acc[:], ACT.Copy, scale=1.0 / RES_GAIN)
+            nc.scalar.activation(sb("z", j)[:, I : I + S], acc[:], ACT.Copy, scale=1.0 / RES_GAIN)
 
         def gather_b(j):
-            tag = "slot0" if j == BLOCKS - 1 else "b%d" % j
-            b_sb[j] = held.tile([P, T], F32, name="b%d" % j, tag=tag, align_bytes=64)
-            for h in range(2):
-                nc.vector.tensor_copy(
-                    b_sb[j][:, h * T // 2 : (h + 1) * T // 2],
-                    zb_sb[j][:].indirect(list_b[:, h * T // 32 : (h + 1) * T // 32]),
-                )
+            nc.vector.tensor_copy(sb("b", j)[:], sb("z", j)[:, I:].indirect(list_b[:]))
 
-        grouped = [held.tile([P, PASSES, P, PACK], BF16, name="grouped%d" % j, tag="slot%d" % j, align_bytes=64) for j in range(BLOCKS)]
+        grouped = [
+            held.tile([P, PASSES, P, PACK], BF16, name="grouped%d" % j, tag="grouped%d" % j, align_bytes=64)
+            for j in range(BLOCKS)
+        ]
         codes = [held.tile([P, PASSES * P], U32, name="codes%d" % j, align_bytes=64) for j in range(BLOCKS)]
         scales = [held.tile([P, PASSES * P], U8, name="scales%d" % j, align_bytes=64) for j in range(BLOCKS)]
 
-        def round_wa(j):
-            src = wa_raw[j // 2][:, :, :, (j % 2) * P : (j % 2 + 1) * P]
-            nc.scalar.copy(
-                grouped[j][:].rearrange("p z (c i) t -> p z c t i", i=4),
-                src.rearrange("p z t (c i) -> p z c t i", i=4),
-            )
+        def round_wa(j, z, on_vector=False):
+            src = wa_raw[j // 2][:, z, :, (j % 2) * P : (j % 2 + 1) * P].rearrange("p t (c i) -> p c t i", i=4)
+            dst = grouped[j][:, z].rearrange("p (c i) t -> p c t i", i=4)
+            if on_vector:
+                nc.vector.tensor_copy(dst, src)
+            else:
+                nc.scalar.activation(dst, src, ACT.Copy)
+
+        def round_both(j):
+            src = wa_raw[j // 2][:, :, :, (j % 2) * P : (j % 2 + 1) * P].rearrange("p z t (c i) -> p z c t i", i=4)
+            nc.scalar.copy(grouped[j][:].rearrange("p z (c i) t -> p z c t i", i=4), src)
 
         def quantize_wa(j):
             nc.vector.quantize_mx(
@@ -129,10 +137,10 @@ def tile_moe_combine_by_larger_kernel(
         acc_a = {}
 
         def product_a(j):
-            acc = psum.tile([P, I], F32, name="acc_a%d" % j, tag="bank%d" % (4 + j % 2))
+            acc_a[j] = psum.tile([P, I], F32, name="acc_a%d" % j, tag="bank%d" % (4, 5, 2, 3)[j])
             for z in range(PASSES):
                 nc.tensor.matmul_mx(
-                    out=acc[:],
+                    out=acc_a[j][:],
                     lhsT=codes[j][:, z * P : (z + 1) * P].bitcast(FP8X4),
                     lhsT_scale=scales[j][:, z * P : (z + 1) * P],
                     rhs=xa_w[:, z, :].bitcast(FP8X4),
@@ -140,87 +148,102 @@ def tile_moe_combine_by_larger_kernel(
                     start=(z == 0),
                     stop=(z == PASSES - 1),
                 )
-            acc_a[j] = acc
 
         def evacuate_a(j):
-            za_sb[j] = held.tile([P, I], F32, name="za%d" % j, tag="raw1" if j == 1 else "za%d" % j)
-            nc.scalar.activation(za_sb[j][:], acc_a[j][:], ACT.Copy, scale=1.0 / RES_GAIN)
+            nc.scalar.activation(sb("z", j)[:, 0:I], acc_a[j][:], ACT.Copy, scale=1.0 / RES_GAIN)
 
         u_ps = {}
+        turned = {}
 
-        def base(j):
-            if j < 2:
-                nc.vector.tensor_tensor(u_sb[j][:], res_sb[j // 2][:, j % 2, :], b_sb[j][:], ALU.add)
-                u_ps[j] = u_sb[j]
-                return
-            turned = psum.tile([P, T], F32, name="turned%d" % j, tag="bank%d" % (6 + j % 2))
+        def turn(j):
+            turned[j] = psum.tile([P, T], F32, name="turned%d" % j, tag="bank%d" % (6, 7, 4, 5)[j])
             for c in range(T // P):
                 cols = slice(c * P, (c + 1) * P)
                 nc.tensor.matmul(
-                    turned[:, cols], res_sb[j // 2][:, j % 2, cols], ident[:], start=True, stop=False, is_transpose=True
+                    turned[j][:, cols], res_sb[j // 2][:, j % 2, cols], ident[:], start=True, stop=False, is_transpose=True
                 )
-                nc.tensor.matmul(turned[:, cols], b_sb[j][:, cols], ident[:], start=False, stop=True, is_transpose=True)
-            nc.scalar.copy(u_sb[j][:], turned[:])
+                nc.tensor.matmul(
+                    turned[j][:, cols], sb("b", j)[:, cols], ident[:], start=False, stop=True, is_transpose=True
+                )
+
+        def back(j):
+            nc.scalar.copy(sb("u", j)[:], turned[j][:])
             u_ps[j] = psum.tile([P, T], F32, name="u_ps%d" % j, tag="bank%d" % j)
             for c in range(T // P):
                 cols = slice(c * P, (c + 1) * P)
-                nc.tensor.transpose(u_ps[j][:, cols], u_sb[j][:, cols], ident[:])
+                nc.tensor.transpose(u_ps[j][:, cols], sb("u", j)[:, cols], ident[:])
 
-        d_sb = {}
-        q_sb = {}
-        q_tags = ("slot3", "q1", "u2", "u3")
+        def base_on_vector(j):
+            nc.vector.tensor_tensor(sb("u", j)[:], res_sb[j // 2][:, j % 2, :], sb("b", j)[:], ALU.add)
+            u_ps[j] = sb("u", j)
 
         def gap(j):
-            d_sb[j] = held.tile([P, T], F32, name="d%d" % j, tag="slot1" if j == 0 else "d%d" % j, align_bytes=64)
-            for h in range(2):
-                cols = slice(h * T // 2, (h + 1) * T // 2)
-                nc.vector.tensor_tensor(
-                    d_sb[j][:, cols],
-                    za_sb[j][:].indirect(list_a[:, h * T // 32 : (h + 1) * T // 32]),
-                    b_sb[j][:, cols],
-                    ALU.subtract,
-                )
-            q_sb[j] = held.tile([P, T], F32, name="q%d" % j, tag=q_tags[j], align_bytes=64)
-            nc.scalar.activation(q_sb[j][:], d_sb[j][:], ACT.Square, scale=0.5 * RES_GAIN)
+            nc.vector.tensor_tensor(sb("d", j)[:], sb("z", j)[:].indirect(list_a[:]), sb("b", j)[:], ALU.subtract)
+
+        def square(j):
+            nc.scalar.activation(sb("q", j)[:], sb("d", j)[:], ACT.Square, scale=0.5 * RES_GAIN)
 
         def larger(j, cols=slice(0, T)):
-            nc.vector.scalar_tensor_tensor(w_sb[j][:, cols], d_sb[j][:, cols], 0.0, u_ps[j][:, cols], ALU.max, ALU.add)
+            nc.vector.scalar_tensor_tensor(
+                sb("w", j)[:, cols], sb("d", j)[:, cols], 0.0, u_ps[j][:, cols], ALU.max, ALU.add
+            )
 
         def finish(j, cols=slice(0, T)):
             nc.vector.scalar_tensor_tensor(
-                y_sb[j][:, cols], w_sb[j][:, cols], RES_GAIN, q_sb[j][:, cols], ALU.mult, ALU.subtract
+                sb("y", j)[:, cols], sb("w", j)[:, cols], RES_GAIN, sb("q", j)[:, cols], ALU.mult, ALU.subtract
             )
-            nc.sync.dma_start(out=out[j * P : (j + 1) * P, cols], in_=y_sb[j][:, cols])
+            nc.sync.dma_start(out=out[j * P : (j + 1) * P, cols], in_=sb("y", j)[:, cols])
 
-        for j in range(BLOCKS - 1):
-            product_b(j)
-            gather_b(j)
-        round_wa(0)
+        left, right = slice(0, T // 2), slice(T // 2, T)
+        round_wa(0, 0)
+        round_wa(1, 0)
+        round_wa(0, 1, True)
+        round_wa(1, 1)
         quantize_wa(0)
-        product_b(BLOCKS - 1)
-        gather_b(BLOCKS - 1)
-        for j in range(1, BLOCKS):
-            round_wa(j)
-            quantize_wa(j)
-            product_a(j - 1)
-            if j == 1:
-                evacuate_a(0)
-        product_a(BLOCKS - 1)
-        for j in range(BLOCKS):
-            if j + 1 < BLOCKS:
-                evacuate_a(j + 1)
-            if j == 0:
-                base(2)
-                base(3)
-            gap(j)
-            if j > 0:
-                finish(j - 1)
-            if j < 2:
-                base(j)
-            if j < BLOCKS - 1:
-                larger(j)
-        halves = (slice(0, T // 2), slice(T // 2, T))
-        for cols in halves:
-            larger(BLOCKS - 1, cols)
-        for cols in halves:
-            finish(BLOCKS - 1, cols)
+        quantize_wa(1)
+        product_b(0)
+        gather_b(0)
+        product_b(1)
+        gather_b(1)
+        product_b(2)
+        gather_b(2)
+        product_b(3)
+        gather_b(3)
+        round_both(2)
+        quantize_wa(2)
+        round_both(3)
+        quantize_wa(3)
+        turn(0)
+        turn(1)
+        product_a(0)
+        evacuate_a(0)
+        product_a(1)
+        evacuate_a(1)
+        product_a(2)
+        evacuate_a(2)
+        product_a(3)
+        turn(2)
+        back(0)
+        evacuate_a(3)
+        back(1)
+        turn(3)
+        back(2)
+        back(3)
+        gap(0)
+        gap(1)
+        gap(2)
+        larger(0)
+        gap(3)
+        square(0)
+        larger(1)
+        finish(0)
+        square(1)
+        larger(2)
+        finish(1)
+        square(2)
+        square(3)
+        larger(3, left)
+        larger(3, right)
+        finish(2)
+        finish(3, left)
+        finish(3, right)

from contextlib import ExitStack

import concourse.mybir as mybir
from concourse.masks import make_identity

K, I, L, S, T, N = 1024, 512, 512, 512, 512, 512
FLOPS = 2 * K * N * I + 2 * L * N * S

F32 = mybir.dt.float32
BF16 = mybir.dt.bfloat16
I32 = mybir.dt.int32
U32 = mybir.dt.uint32
U16 = mybir.dt.uint16
U8 = mybir.dt.uint8
FP8X4 = mybir.dt.float8_e4m3fn_x4
FP4X4 = mybir.dt.float4_e2m1fn_x4
ALU = mybir.AluOpType
ACT = mybir.ActivationFunctionType

P = 128
PACK = 4
K_PASS = P * PACK
PASSES = K // K_PASS
BLOCKS = N // P
HALF = N // 2
RES_GAIN = 0.3
SPARE = 192


def tile_moe_combine_by_larger_kernel(
    tc, xa_words, xa_scales, wa, xb_words, xb_scales, wb_words, wb_scales, res, offs, offs2, out
):
    nc = tc.nc
    with ExitStack() as ctx:
        held = ctx.enter_context(tc.tile_pool(name="held", bufs=1))
        psum = ctx.enter_context(tc.psum_pool(name="psum", bufs=1))

        list_a = held.tile([P, T // 16], U16, name="list_a")
        list_b = held.tile([P, T // 16], U16, name="list_b")
        wb_w = held.tile([P, PACK * N], U8, name="wb_w", align_bytes=64)
        xb_w = held.tile([P, 2 * S], U8, name="xb_w", align_bytes=64)
        xa_w = held.tile([P, PASSES, PACK * I], U8, name="xa_w", align_bytes=64)
        b_planes = held.tile([P, N + S], U8, name="b_planes", align_bytes=64)
        xa_s = held.tile([P, PASSES, I], U8, name="xa_s", align_bytes=64)
        wa_raw = [held.tile([P, PASSES, PACK, HALF], F32, name="wa_raw%d" % h, tag="raw%d" % h, align_bytes=64) for h in range(2)]
        res_sb = [held.tile([P, 2, T], F32, name="res%d" % h) for h in range(2)]

        ident = held.tile([P, P], F32, name="ident")
        nc.vector.memset(b_planes[:].bitcast(I32), 0)
        nc.vector.memset(xa_s[:].rearrange("p z c -> p (z c)").bitcast(I32), 0)
        make_identity(nc, ident[:])

        def load_words_b():
            nc.sync.dma_start(out=wb_w[:].bitcast(I32), in_=wb_words[0].rearrange("p n r -> p (n r)").bitcast(I32))
            nc.sync.dma_start(out=xb_w[:].bitcast(I32), in_=xb_words[0].bitcast(I32))

        def load_scale_rows(plane, rows, queues=(nc.sync,) * 4):
            for r in range(4):
                queues[r].dma_start(out=plane[r:P:32].bitcast(I32), in_=rows[r:16:4].bitcast(I32))

        def load_wa(h, z):
            rows = wa[z * K_PASS : (z + 1) * K_PASS, h * HALF : (h + 1) * HALF]
            nc.sync.dma_start(out=wa_raw[h][:, z, :, :], in_=rows.rearrange("(p j) n -> p j n", j=PACK))

        def load_res(h):
            rows = res[h * HALF : (h + 1) * HALF, :]
            nc.sync.dma_start(out=res_sb[h][:], in_=rows.rearrange("(j p) t -> p j t", p=P))

        load_words_b()
        load_scale_rows(b_planes[:, 0:N], wb_scales[0])
        load_wa(0, 0)
        load_wa(0, 1)
        load_scale_rows(b_planes[:, N : N + S], xb_scales[0])
        nc.sync.dma_start(list_b[:], offs2)
        load_wa(1, 0)
        load_res(0)
        load_wa(1, 1)
        nc.sync.dma_start(out=xa_w[:].bitcast(I32), in_=xa_words.rearrange("z p c r -> p z (c r)").bitcast(I32))
        load_scale_rows(xa_s[:], xa_scales.rearrange("z q c -> q z c"))
        nc.sync.dma_start(list_a[:], offs)
        load_res(1)

        tags = {"u0":"codes1","u1":"codes3","q0":"codes3","q1":"u2","q2":"u3","q3":"d2"}
        tiles = {}

        def sb(name, j, width=T):
            key = "%s%d" % (name, j)
            if key not in tiles:
                tiles[key] = held.tile([P, width], F32, name=key, tag=tags.get(key, key), align_bytes=64)
            return tiles[key]

        for j in range(BLOCKS):
            nc.gpsimd.memset(sb("z", j, I + S + SPARE)[:, I + S :], 0.0)

        def product_b(j):
            acc = psum.tile([P, S], F32, name="acc_b%d" % j, tag="bank%d" % j)
            nc.tensor.matmul_mx(
                out=acc[:],
                lhsT=wb_w[:, j * PACK * P : (j + 1) * PACK * P].bitcast(FP8X4),
                lhsT_scale=b_planes[:, j * P : (j + 1) * P],
                rhs=xb_w[:].bitcast(FP4X4),
                rhs_scale=b_planes[:, N : N + S],
                start=True,
                stop=True,
            )
            nc.scalar.activation(sb("z", j)[:, I : I + S], acc[:], ACT.Copy, scale=1.0 / RES_GAIN)

        def gather_b(j):
            nc.vector.tensor_copy(sb("b", j)[:], sb("z", j)[:, I:].indirect(list_b[:]))

        grouped = [
            held.tile([P, PASSES, P, PACK], BF16, name="grouped%d" % j, tag="grouped%d" % j, align_bytes=64)
            for j in range(BLOCKS)
        ]
        codes = [held.tile([P, PASSES * P], U32, name="codes%d" % j, align_bytes=64) for j in range(BLOCKS)]
        scales = [held.tile([P, PASSES * P], U8, name="scales%d" % j, align_bytes=64) for j in range(BLOCKS)]

        def round_wa(j, z, on_vector=False):
            src = wa_raw[j // 2][:, z, :, (j % 2) * P : (j % 2 + 1) * P].rearrange("p t (c i) -> p c t i", i=4)
            dst = grouped[j][:, z].rearrange("p (c i) t -> p c t i", i=4)
            if on_vector:
                nc.vector.tensor_copy(dst, src)
            else:
                nc.scalar.activation(dst, src, ACT.Copy)

        def round_both(j):
            src = wa_raw[j // 2][:, :, :, (j % 2) * P : (j % 2 + 1) * P].rearrange("p z t (c i) -> p z c t i", i=4)
            nc.scalar.copy(grouped[j][:].rearrange("p z (c i) t -> p z c t i", i=4), src)

        def quantize_wa(j):
            nc.vector.quantize_mx(
                out=codes[j][:].bitcast(FP8X4),
                scales=scales[j][:],
                in_=grouped[j][:].rearrange("p z n t -> p (z n t)"),
            )

        acc_a = {}

        def product_a(j):
            acc_a[j] = psum.tile([P, I], F32, name="acc_a%d" % j, tag="bank%d" % (4, 5, 2, 3)[j])
            for z in range(PASSES):
                nc.tensor.matmul_mx(
                    out=acc_a[j][:],
                    lhsT=codes[j][:, z * P : (z + 1) * P].bitcast(FP8X4),
                    lhsT_scale=scales[j][:, z * P : (z + 1) * P],
                    rhs=xa_w[:, z, :].bitcast(FP8X4),
                    rhs_scale=xa_s[:, z, :],
                    start=(z == 0),
                    stop=(z == PASSES - 1),
                )

        def evacuate_a(j):
            nc.scalar.activation(sb("z", j)[:, 0:I], acc_a[j][:], ACT.Copy, scale=1.0 / RES_GAIN)

        u_ps = {}
        turned = {}

        def turn(j):
            turned[j] = psum.tile([P, T], F32, name="turned%d" % j, tag="bank%d" % (6, 7, 4, 5)[j])
            for c in range(T // P):
                cols = slice(c * P, (c + 1) * P)
                nc.tensor.matmul(
                    turned[j][:, cols], res_sb[j // 2][:, j % 2, cols], ident[:], start=True, stop=False, is_transpose=True
                )
                nc.tensor.matmul(
                    turned[j][:, cols], sb("b", j)[:, cols], ident[:], start=False, stop=True, is_transpose=True
                )

        def back(j):
            nc.scalar.copy(sb("u", j)[:], turned[j][:])
            u_ps[j] = psum.tile([P, T], F32, name="u_ps%d" % j, tag="bank%d" % j)
            for c in range(T // P):
                cols = slice(c * P, (c + 1) * P)
                nc.tensor.transpose(u_ps[j][:, cols], sb("u", j)[:, cols], ident[:])

        def base_on_vector(j):
            nc.vector.tensor_tensor(sb("u", j)[:], res_sb[j // 2][:, j % 2, :], sb("b", j)[:], ALU.add)
            u_ps[j] = sb("u", j)

        def gap(j):
            nc.vector.tensor_tensor(sb("d", j)[:], sb("z", j)[:].indirect(list_a[:]), sb("b", j)[:], ALU.subtract)

        def square(j):
            nc.scalar.activation(sb("q", j)[:], sb("d", j)[:], ACT.Square, scale=0.5 * RES_GAIN)

        def larger(j, cols=slice(0, T)):
            nc.vector.scalar_tensor_tensor(
                sb("w", j)[:, cols], sb("d", j)[:, cols], 0.0, u_ps[j][:, cols], ALU.max, ALU.add
            )

        def finish(j, cols=slice(0, T)):
            nc.vector.scalar_tensor_tensor(
                sb("y", j)[:, cols], sb("w", j)[:, cols], RES_GAIN, sb("q", j)[:, cols], ALU.mult, ALU.subtract
            )
            nc.sync.dma_start(out=out[j * P : (j + 1) * P, cols], in_=sb("y", j)[:, cols])

        left, right = slice(0, T // 2), slice(T // 2, T)
        round_wa(0, 0)
        round_wa(1, 0)
        round_wa(0, 1, True)
        round_wa(1, 1)
        quantize_wa(0)
        quantize_wa(1)
        product_b(0)
        gather_b(0)
        product_b(1)
        gather_b(1)
        product_b(2)
        gather_b(2)
        product_b(3)
        gather_b(3)
        round_both(2)
        quantize_wa(2)
        round_both(3)
        quantize_wa(3)
        turn(0)
        turn(1)
        product_a(0)
        evacuate_a(0)
        product_a(1)
        evacuate_a(1)
        product_a(2)
        evacuate_a(2)
        product_a(3)
        turn(2)
        back(0)
        evacuate_a(3)
        back(1)
        turn(3)
        back(2)
        back(3)
        gap(0)
        gap(1)
        gap(2)
        larger(0)
        gap(3)
        square(0)
        larger(1)
        finish(0)
        square(1)
        larger(2)
        finish(1)
        square(2)
        square(3)
        larger(3, left)
        larger(3, right)
        finish(2)
        finish(3, left)
        finish(3, right)
